import numpy as np, ml_dtypes
CORES = [0,1,2,3,128,129,130,131,256,257,258,259,384,385,386,387]
N = 16
def setup_inputs(rng):
    return {"x": rng.standard_normal((N, 128, 128), dtype=np.float32).astype(ml_dtypes.bfloat16)}
def reference(x):
    g = np.concatenate(list(x), axis=1)
    return {"y": np.broadcast_to(g, (N,) + g.shape)}

@@ -1,0 +1,45 @@
+import concourse.bass as bass
+
+W = 128
+SCRATCH = {"land": ("sbuf", [128, 16 * W], "bfloat16")}
+SEMAPHORES = ["ld", "st", "own", "in_s", "in_c", "in_d", "nb_s", "nb_c", "nb_d", "sent"]
+
+
+def rank_program(g, core, T, topo):
+    if T.rank_of(core) is None:
+        return
+    h, i = topo.host(core), core % 8
+    s, c = h ^ 1, 3 - h
+    d = 3 - s
+    S = T.sem
+
+    def to(q):
+        rid, pid = topo.addr(q, core)
+        return bass.DstId(rid=rid, pnc=pid)
+
+    def piece(host):
+        a = (4 * host + i) * W
+        return T.land[:, a:a + W]
+
+    peers = [to(128 * h + j) for j in range(4) if j != i]
+
+    def spread(src, sem):
+        return bass.RemoteDMATransfer(dst_ids=peers, dma_engine_mask=0xFF00, remote_sem=sem, srcs=[src], dsts=[src] * 3)
+
+    def away(src, host, sem, mask):
+        return bass.RemoteDMATransfer(dst_ids=[to(128 * host + i)], dma_engine_mask=mask, remote_sem=sem, srcs=[src], dsts=[src])
+
+    g.dma_start(piece(h), T.x[:]).then_inc(S.ld, 16)
+    g.wait_ge(S.ld, 16)
+    g.remote_dma_fused([away(piece(h), c, S.in_c, 0x000F), away(piece(h), s, S.in_s, 0x00F0), spread(piece(h), S.own)], local_sem=S.sent)
+    g.wait_ge(S.in_c, 4)
+    g.remote_dma_fused([away(piece(c), s, S.in_d, 0x00FF), spread(piece(c), S.nb_c)], local_sem=S.sent)
+    g.wait_ge(S.in_s, 4)
+    g.remote_dma_fused([spread(piece(s), S.nb_s)], local_sem=S.sent)
+    g.wait_ge(S.in_d, 8)
+    g.remote_dma_fused([spread(piece(d), S.nb_d)], local_sem=S.sent)
+    for sem in (S.own, S.nb_c, S.nb_s, S.nb_d):
+        g.wait_ge(sem, 24)
+    g.dma_start(T.y[:], T.land[:]).then_inc(S.st, 16)
+    g.wait_ge(S.st, 16)
+    g.wait_ge(S.sent, 16 + 16 + 8 + 8)

@@ -29,6 +29,10 @@ def rank_program(g, core, T, topo):
     def away(src, host, sem, mask):
         return bass.RemoteDMATransfer(dst_ids=[to(128 * host + i)], dma_engine_mask=mask, remote_sem=sem, srcs=[src], dsts=[src])
 
+    def store(host):
+        a = 4 * host * W
+        g.dma_start(T.y[:, a:a + 4 * W], T.land[:, a:a + 4 * W]).then_inc(S.st, 16)
+
     g.dma_start(piece(h), T.x[:]).then_inc(S.ld, 16)
     g.wait_ge(S.ld, 16)
     g.remote_dma_fused([away(piece(h), c, S.in_c, 0x000F), away(piece(h), s, S.in_s, 0x00F0), spread(piece(h), S.own)], local_sem=S.sent)
@@ -36,10 +40,15 @@ def rank_program(g, core, T, topo):
     g.remote_dma_fused([away(piece(c), s, S.in_d, 0x00FF), spread(piece(c), S.nb_c)], local_sem=S.sent)
     g.wait_ge(S.in_s, 4)
     g.remote_dma_fused([spread(piece(s), S.nb_s)], local_sem=S.sent)
+    g.wait_ge(S.own, 24)
+    store(h)
     g.wait_ge(S.in_d, 8)
     g.remote_dma_fused([spread(piece(d), S.nb_d)], local_sem=S.sent)
-    for sem in (S.own, S.nb_c, S.nb_s, S.nb_d):
-        g.wait_ge(sem, 24)
-    g.dma_start(T.y[:], T.land[:]).then_inc(S.st, 16)
-    g.wait_ge(S.st, 16)
+    g.wait_ge(S.nb_c, 24)
+    store(c)
+    g.wait_ge(S.nb_s, 24)
+    store(s)
+    g.wait_ge(S.nb_d, 24)
+    store(d)
+    g.wait_ge(S.st, 64)
     g.wait_ge(S.sent, 16 + 16 + 8 + 8)

@@ -2,53 +2,68 @@ import concourse.bass as bass
 
 W = 128
 SCRATCH = {"land": ("sbuf", [128, 16 * W], "bfloat16")}
-SEMAPHORES = ["ld", "st", "own", "in_s", "in_c", "in_d", "nb_s", "nb_c", "nb_d", "sent"]
+SEMAPHORES = ["ld", "st", "own", "fin", "nb_s", "nb_c", "dg", "sent"]
 
 
 def rank_program(g, core, T, topo):
-    if T.rank_of(core) is None:
+    if topo.chip(core) != 0:
         return
-    h, i = topo.host(core), core % 8
+    h, k = topo.host(core), core % 8
     s, c = h ^ 1, 3 - h
     d = 3 - s
     S = T.sem
+    i = k % 4
+    takes_c = (k < 4) == (i % 2 == 0)
 
-    def to(q):
-        rid, pid = topo.addr(q, core)
+    def to(host, j):
+        rid, pid = topo.addr(128 * host + j, core)
         return bass.DstId(rid=rid, pnc=pid)
 
-    def piece(host):
-        a = (4 * host + i) * W
+    def piece(host, j):
+        a = (4 * host + j) * W
         return T.land[:, a:a + W]
 
-    peers = [to(128 * h + j) for j in range(4) if j != i]
+    def tr(src, dsts, mask, sem):
+        return bass.RemoteDMATransfer(dst_ids=dsts, dma_engine_mask=mask, remote_sem=sem, srcs=[src], dsts=[src] * len(dsts))
 
-    def spread(src, sem):
-        return bass.RemoteDMATransfer(dst_ids=peers, dma_engine_mask=0xFF00, remote_sem=sem, srcs=[src], dsts=[src] * 3)
+    here = [to(h, j) for j in range(4) if j != k]
 
-    def away(src, host, sem, mask):
-        return bass.RemoteDMATransfer(dst_ids=[to(128 * host + i)], dma_engine_mask=mask, remote_sem=sem, srcs=[src], dsts=[src])
+    def pass_on():
+        g.wait_ge(S.fin, 4)
+        if takes_c:
+            g.remote_dma_fused([tr(piece(c, i), [to(s, j) for j in range(4)], 0x00FF, S.dg),
+                                tr(piece(c, i), here, 0xFF00, S.nb_c)], local_sem=S.sent)
+        else:
+            g.remote_dma_fused([tr(piece(s, i), here, 0xFFFF, S.nb_s)], local_sem=S.sent)
+
+    if k >= 4:
+        pass_on()
+        g.wait_ge(S.sent, 16)
+        return
 
     def store(host):
         a = 4 * host * W
         g.dma_start(T.y[:, a:a + 4 * W], T.land[:, a:a + 4 * W]).then_inc(S.st, 16)
 
-    g.dma_start(piece(h), T.x[:]).then_inc(S.ld, 16)
+    mine = piece(h, k)
+    g.dma_start(mine, T.x[:]).then_inc(S.ld, 16)
     g.wait_ge(S.ld, 16)
-    g.remote_dma_fused([away(piece(h), c, S.in_c, 0x000F), away(piece(h), s, S.in_s, 0x00F0), spread(piece(h), S.own)], local_sem=S.sent)
-    g.wait_ge(S.in_c, 4)
-    g.remote_dma_fused([away(piece(c), s, S.in_d, 0x00FF), spread(piece(c), S.nb_c)], local_sem=S.sent)
-    g.wait_ge(S.in_s, 4)
-    g.remote_dma_fused([spread(piece(s), S.nb_s)], local_sem=S.sent)
-    g.wait_ge(S.own, 24)
-    store(h)
-    g.wait_ge(S.in_d, 8)
-    g.remote_dma_fused([spread(piece(d), S.nb_d)], local_sem=S.sent)
-    g.wait_ge(S.nb_c, 24)
-    store(c)
-    g.wait_ge(S.nb_s, 24)
+    g.remote_dma_fused([tr(mine, [to(c, k if k % 2 == 0 else 4 + k)], 0x000F, S.fin),
+                        tr(mine, [to(s, 4 + k if k % 2 == 0 else k)], 0x00F0, S.fin),
+                        tr(mine, here, 0xFF00, S.own)], local_sem=S.sent)
+    if takes_c:
+        g.wait_ge(S.own, 24)
+        store(h)
+        pass_on()
+    else:
+        pass_on()
+        g.wait_ge(S.own, 24)
+        store(h)
+    g.wait_ge(S.nb_s, 64 if takes_c else 48)
     store(s)
-    g.wait_ge(S.nb_d, 24)
+    g.wait_ge(S.nb_c, 24 if takes_c else 32)
+    store(c)
+    g.wait_ge(S.dg, 32)
     store(d)
     g.wait_ge(S.st, 64)
-    g.wait_ge(S.sent, 16 + 16 + 8 + 8)
+    g.wait_ge(S.sent, 32)

@@ -10,7 +10,6 @@ def rank_program(g, core, T, topo):
         return
     h, k = topo.host(core), core % 8
     s, c = h ^ 1, 3 - h
-    d = 3 - s
     S = T.sem
     i = k % 4
     takes_c = (k < 4) == (i % 2 == 0)
@@ -41,9 +40,9 @@ def rank_program(g, core, T, topo):
         g.wait_ge(S.sent, 16)
         return
 
-    def store(host):
-        a = 4 * host * W
-        g.dma_start(T.y[:, a:a + 4 * W], T.land[:, a:a + 4 * W]).then_inc(S.st, 16)
+    def store(rack):
+        a = 8 * rack * W
+        g.dma_start(T.y[:, a:a + 8 * W], T.land[:, a:a + 8 * W]).then_inc(S.st, 16)
 
     mine = piece(h, k)
     g.dma_start(mine, T.x[:]).then_inc(S.ld, 16)
@@ -51,19 +50,12 @@ def rank_program(g, core, T, topo):
     g.remote_dma_fused([tr(mine, [to(c, k if k % 2 == 0 else 4 + k)], 0x000F, S.fin),
                         tr(mine, [to(s, 4 + k if k % 2 == 0 else k)], 0x00F0, S.fin),
                         tr(mine, here, 0xFF00, S.own)], local_sem=S.sent)
-    if takes_c:
-        g.wait_ge(S.own, 24)
-        store(h)
-        pass_on()
-    else:
-        pass_on()
-        g.wait_ge(S.own, 24)
-        store(h)
+    pass_on()
+    g.wait_ge(S.own, 24)
     g.wait_ge(S.nb_s, 64 if takes_c else 48)
-    store(s)
+    store(h // 2)
     g.wait_ge(S.nb_c, 24 if takes_c else 32)
-    store(c)
     g.wait_ge(S.dg, 32)
-    store(d)
-    g.wait_ge(S.st, 64)
+    store(c // 2)
+    g.wait_ge(S.st, 32)
     g.wait_ge(S.sent, 32)

@@ -2,7 +2,7 @@ import concourse.bass as bass
 
 W = 128
 SCRATCH = {"land": ("sbuf", [128, 16 * W], "bfloat16")}
-SEMAPHORES = ["ld", "st", "own", "fin", "nb_s", "nb_c", "dg", "sent"]
+SEMAPHORES = ["ld", "st", "own", "hop", "fin", "nb_s", "nb_c", "dg", "sent"]
 
 
 def rank_program(g, core, T, topo):
@@ -28,7 +28,7 @@ def rank_program(g, core, T, topo):
     here = [to(h, j) for j in range(4) if j != k]
 
     def pass_on():
-        g.wait_ge(S.fin, 4)
+        g.wait_ge(S.fin, 8 if k in (5, 7) else 4)
         if takes_c:
             g.remote_dma_fused([tr(piece(c, i), [to(s, j) for j in range(4)], 0x00FF, S.dg),
                                 tr(piece(c, i), here, 0xFF00, S.nb_c)], local_sem=S.sent)
@@ -36,8 +36,11 @@ def rank_program(g, core, T, topo):
             g.remote_dma_fused([tr(piece(s, i), here, 0xFFFF, S.nb_s)], local_sem=S.sent)
 
     if k >= 4:
+        if takes_c:
+            g.wait_ge(S.hop, 4)
+            g.remote_dma_fused([tr(piece(h, i), [to(c, k)], 0x00FF, S.fin)], local_sem=S.sent)
         pass_on()
-        g.wait_ge(S.sent, 16)
+        g.wait_ge(S.sent, 24 if takes_c else 16)
         return
 
     def store(rack):
@@ -47,9 +50,14 @@ def rank_program(g, core, T, topo):
     mine = piece(h, k)
     g.dma_start(mine, T.x[:]).then_inc(S.ld, 16)
     g.wait_ge(S.ld, 16)
-    g.remote_dma_fused([tr(mine, [to(c, k if k % 2 == 0 else 4 + k)], 0x000F, S.fin),
-                        tr(mine, [to(s, 4 + k if k % 2 == 0 else k)], 0x00F0, S.fin),
-                        tr(mine, here, 0xFF00, S.own)], local_sem=S.sent)
+    if k % 2 == 0:
+        g.remote_dma_fused([tr(mine, [to(c, k)], 0x000F, S.fin),
+                            tr(mine, [to(s, 4 + k)], 0x00F0, S.fin),
+                            tr(mine, here, 0xFF00, S.own)], local_sem=S.sent)
+    else:
+        g.remote_dma_fused([tr(mine, [to(h, 4 + k)], 0x000F, S.hop),
+                            tr(mine, [to(s, k)], 0x00F0, S.fin),
+                            tr(mine, here, 0xFF00, S.own)], local_sem=S.sent)
     pass_on()
     g.wait_ge(S.own, 24)
     g.wait_ge(S.nb_s, 64 if takes_c else 48)

@@ -12,7 +12,6 @@ def rank_program(g, core, T, topo):
     s, c = h ^ 1, 3 - h
     S = T.sem
     i = k % 4
-    takes_c = (k < 4) == (i % 2 == 0)
 
     def to(host, j):
         rid, pid = topo.addr(128 * host + j, core)
@@ -25,22 +24,17 @@ def rank_program(g, core, T, topo):
     def tr(src, dsts, mask, sem):
         return bass.RemoteDMATransfer(dst_ids=dsts, dma_engine_mask=mask, remote_sem=sem, srcs=[src], dsts=[src] * len(dsts))
 
-    here = [to(h, j) for j in range(4) if j != k]
-
-    def pass_on():
-        g.wait_ge(S.fin, 8 if k in (5, 7) else 4)
-        if takes_c:
-            g.remote_dma_fused([tr(piece(c, i), [to(s, j) for j in range(4)], 0x00FF, S.dg),
-                                tr(piece(c, i), here, 0xFF00, S.nb_c)], local_sem=S.sent)
-        else:
-            g.remote_dma_fused([tr(piece(s, i), here, 0xFFFF, S.nb_s)], local_sem=S.sent)
+    def ranks(host):
+        return [to(host, j) for j in range(4) if (host, j) != (h, k)]
 
     if k >= 4:
-        if takes_c:
+        if i % 2:
             g.wait_ge(S.hop, 4)
             g.remote_dma_fused([tr(piece(h, i), [to(c, k)], 0x00FF, S.fin)], local_sem=S.sent)
-        pass_on()
-        g.wait_ge(S.sent, 24 if takes_c else 16)
+        g.wait_ge(S.fin, 8 if i % 2 else 4)
+        g.remote_dma_fused([tr(piece(c, i), ranks(s), 0x00FF, S.dg),
+                            tr(piece(c, i), ranks(h), 0xFF00, S.nb_c)], local_sem=S.sent)
+        g.wait_ge(S.sent, 24 if i % 2 else 16)
         return
 
     def store(rack):
@@ -50,20 +44,14 @@ def rank_program(g, core, T, topo):
     mine = piece(h, k)
     g.dma_start(mine, T.x[:]).then_inc(S.ld, 16)
     g.wait_ge(S.ld, 16)
-    if k % 2 == 0:
-        g.remote_dma_fused([tr(mine, [to(c, k)], 0x000F, S.fin),
-                            tr(mine, [to(s, 4 + k)], 0x00F0, S.fin),
-                            tr(mine, here, 0xFF00, S.own)], local_sem=S.sent)
-    else:
-        g.remote_dma_fused([tr(mine, [to(h, 4 + k)], 0x000F, S.hop),
-                            tr(mine, [to(s, k)], 0x00F0, S.fin),
-                            tr(mine, here, 0xFF00, S.own)], local_sem=S.sent)
-    pass_on()
+    g.remote_dma_fused([tr(mine, [to(c, 4 + k)], 0x000F, S.fin) if k % 2 == 0 else tr(mine, [to(h, 4 + k)], 0x000F, S.hop),
+                        tr(mine, ranks(s), 0x00F0, S.nb_s),
+                        tr(mine, ranks(h), 0xFF00, S.own)], local_sem=S.sent)
     g.wait_ge(S.own, 24)
-    g.wait_ge(S.nb_s, 64 if takes_c else 48)
+    g.wait_ge(S.nb_s, 16)
     store(h // 2)
-    g.wait_ge(S.nb_c, 24 if takes_c else 32)
+    g.wait_ge(S.nb_c, 32)
     g.wait_ge(S.dg, 32)
     store(c // 2)
     g.wait_ge(S.st, 32)
-    g.wait_ge(S.sent, 32)
+    g.wait_ge(S.sent, 16)

import concourse.bass as bass

W = 128
SCRATCH = {"land": ("sbuf", [128, 16 * W], "bfloat16")}
SEMAPHORES = ["ld", "st", "own", "hop", "fin", "nb_s", "nb_c", "dg", "sent"]


def rank_program(g, core, T, topo):
    if topo.chip(core) != 0:
        return
    h, k = topo.host(core), core % 8
    s, c = h ^ 1, 3 - h
    S = T.sem
    i = k % 4

    def to(host, j):
        rid, pid = topo.addr(128 * host + j, core)
        return bass.DstId(rid=rid, pnc=pid)

    def piece(host, j):
        a = (4 * host + j) * W
        return T.land[:, a:a + W]

    def tr(src, dsts, mask, sem):
        return bass.RemoteDMATransfer(dst_ids=dsts, dma_engine_mask=mask, remote_sem=sem, srcs=[src], dsts=[src] * len(dsts))

    def ranks(host):
        return [to(host, j) for j in range(4) if (host, j) != (h, k)]

    if k >= 4:
        if i % 2:
            g.wait_ge(S.hop, 4)
            g.remote_dma_fused([tr(piece(h, i), [to(c, k)], 0x00FF, S.fin)], local_sem=S.sent)
        g.wait_ge(S.fin, 8 if i % 2 else 4)
        g.remote_dma_fused([tr(piece(c, i), ranks(s), 0x00FF, S.dg),
                            tr(piece(c, i), ranks(h), 0xFF00, S.nb_c)], local_sem=S.sent)
        g.wait_ge(S.sent, 24 if i % 2 else 16)
        return

    def store(rack):
        a = 8 * rack * W
        g.dma_start(T.y[:, a:a + 8 * W], T.land[:, a:a + 8 * W]).then_inc(S.st, 16)

    mine = piece(h, k)
    g.dma_start(mine, T.x[:]).then_inc(S.ld, 16)
    g.wait_ge(S.ld, 16)
    g.remote_dma_fused([tr(mine, [to(c, 4 + k)], 0x000F, S.fin) if k % 2 == 0 else tr(mine, [to(h, 4 + k)], 0x000F, S.hop),
                        tr(mine, ranks(s), 0x00F0, S.nb_s),
                        tr(mine, ranks(h), 0xFF00, S.own)], local_sem=S.sent)
    g.wait_ge(S.own, 24)
    g.wait_ge(S.nb_s, 16)
    store(h // 2)
    g.wait_ge(S.nb_c, 32)
    g.wait_ge(S.dg, 32)
    store(c // 2)
    g.wait_ge(S.st, 32)
    g.wait_ge(S.sent, 16)
